import numpy as np
import ml_dtypes


def mxq(x, axis, fmt="e4m3"):
    dtype, down = {"e4m3": (ml_dtypes.float8_e4m3fn, 7), "e5m2": (ml_dtypes.float8_e5m2, 14)}[fmt]
    v = np.moveaxis(np.asarray(x, np.float32).astype(ml_dtypes.bfloat16).astype(np.float64), axis, -1)
    blocks = v.reshape(v.shape[:-1] + (-1, 32))
    amax = np.abs(blocks).max(-1, keepdims=True)
    byte = np.maximum(np.where(amax > 0, np.frexp(amax)[1] - 1 + 127, 0) - down, 1)
    scale = np.exp2(byte - 127.0)
    codes = (blocks / scale).astype(np.float32).astype(dtype).astype(np.float64)
    return np.moveaxis((codes * scale).reshape(v.shape), -1, axis)


WIDE = False


def mx_kscale(k):
    if not WIDE:
        return np.ones(k)
    levels = np.array([10, -10, 5, -5, 0])
    if k % 512:
        return np.exp2(np.random.permutation(np.resize(levels, k // 32))).repeat(32)
    a = np.empty((k // 512, 16))
    for p in range(k // 512):
        a[p, :8] = np.random.permutation(np.resize(levels, 8))
        for g in range(8):
            far = levels[np.abs(levels - a[p, g]) >= 10]
            a[p, g + 8] = far[np.random.randint(len(far))]
    return np.exp2(a.ravel()).repeat(32)


def f64(x):
    return np.asarray(x).astype(np.float64)


def striped(idx):
    return np.tile(idx.reshape(-1, 16).T, (8, 1)).astype(np.uint16)


def unstriped(offs):
    return offs[:16].T.reshape(-1).astype(np.int64)


def pack_weight(w):
    k, n = w.shape
    w = f64(np.asarray(w, np.float32).astype(ml_dtypes.bfloat16)).reshape(k // 32, 32, n)
    amax = np.abs(w).max(1)
    byte = np.clip(np.where(amax > 0, np.frexp(amax)[1] - 1 + 127 - 7, 1), 1, 254)
    scaled = (w * np.exp2(127.0 - byte)[:, None, :]).reshape(k, n).astype(np.float32)
    words = np.ascontiguousarray(scaled.reshape(k // 512, 128, 4, n).transpose(0, 1, 3, 2)).astype(ml_dtypes.float8_e4m3fn).view(np.uint8)
    return words, np.ascontiguousarray(byte.astype(np.uint8).reshape(k // 512, 16, n))


def unpack_weight(words, scales):
    g, p, n, _ = words.shape
    vals = np.ascontiguousarray(words).view(ml_dtypes.float8_e4m3fn).astype(np.float64) * np.repeat(np.exp2(scales.astype(np.float64) - 127.0), 8, axis=1)[..., None]
    return vals.transpose(0, 1, 3, 2).reshape(g * 512, n)


def relu(v):
    return np.maximum(v, 0.0)


K, T, E, C, N = 512, 2048, 4, 256, 256


def by_expert(wq, xq):
    return np.concatenate([wq[e].T @ xq[:, e * C:(e + 1) * C] for e in range(E)], axis=1)


def setup_inputs():
    n = np.random.standard_normal
    s = mx_kscale(K)[:, None]
    packed = [pack_weight(m) for m in n((E, K, N)) / np.sqrt(K) / s[None]]
    return {
        "xT": (n((K, T)) * s).astype(np.float32),
        "w_words": np.stack([m[0] for m in packed]),
        "w_scales": np.stack([m[1] for m in packed]),
        "b": (0.3 * n((N, E))).astype(np.float32),
        "offs": striped(np.random.permutation(T)[:E * C]),
    }


def reference(xT, w_words, w_scales, b, offs):
    idx = unstriped(offs)
    xq = mxq(f64(xT)[:, idx], 0, "e4m3")
    w = np.stack([unpack_weight(w_words[e], w_scales[e]) for e in range(E)])
    y = by_expert(w, xq)
    y = relu(y + np.repeat(f64(b), C, axis=1))
    out = np.zeros((N, T))
    out[:, idx] = y
    return out

@@ -1,0 +1,163 @@
+from contextlib import ExitStack
+
+import concourse.mybir as mybir
+
+K, T, E, C, N = 512, 2048, 4, 256, 256
+FLOPS = 2 * K * N * E * C
+
+F32 = mybir.dt.float32
+BF16 = mybir.dt.bfloat16
+U32 = mybir.dt.uint32
+I32 = mybir.dt.int32
+U16 = mybir.dt.uint16
+U8 = mybir.dt.uint8
+FP8X4 = mybir.dt.float8_e4m3fn_x4
+RELU = mybir.ActivationFunctionType.Relu
+
+P = 128
+SLOTS = E * C
+OC = C // 16
+
+
+def tile_routed_moe_kernel(tc, xT, w_words, w_scales, b, offs, out):
+    nc = tc.nc
+    with ExitStack() as ctx:
+        held = ctx.enter_context(tc.tile_pool(name="held", bufs=1))
+        psum = ctx.enter_context(tc.psum_pool(name="psum", bufs=1))
+
+        offs_t = held.tile([P, SLOTS // 16], U16, name="offs_t")
+        nc.sync.dma_start(offs_t[:], offs)
+
+        xv = xT.rearrange("(p j) t -> p j t", j=4)
+        plane = []
+        for j in range(4):
+            pl = held.tile([P, T], F32, name="plane%d" % j)
+            nc.sync.dma_start(out=pl[:], in_=xv[:, j, :])
+            plane.append(pl)
+
+        warm = held.tile([P, 2], F32, name="warm")
+        nc.vector.memset(warm[:], 0.0)
+        nc.scalar.activation(warm[:, 1:2], warm[:, 0:1], RELU)
+        w_scl = held.tile([P, E * N], U8, name="w_scl", align_bytes=64)
+        nc.vector.memset(w_scl[:].bitcast(I32), 0)
+
+        w_cod = [held.tile([P, N], I32, name="w_cod%d" % e, align_bytes=64) for e in range(E)]
+
+        def load_w(e):
+            nc.sync.dma_start(out=w_cod[e][:], in_=w_words[e, 0].rearrange("p n r -> p (n r)").bitcast(I32))
+
+        load_w(0)
+        sv = w_scales.rearrange("e a (q r) n -> r q e (a n)", r=4)
+        for r in range(4):
+            nc.sync.dma_start(
+                out=w_scl[r:P:32, :].bitcast(I32).rearrange("q (e n) -> q e n", e=E),
+                in_=sv[r].bitcast(I32),
+            )
+        bias = held.tile([P, 2 * E], F32, name="bias")
+        nc.sync.dma_start(
+            out=bias[:].rearrange("p (h e) -> p h e", h=2),
+            in_=b.rearrange("(h p) e -> p h e", p=P),
+        )
+        for e in range(1, E):
+            load_w(e)
+
+        win = []
+        for h in range(2):
+            wt = held.tile([P, T], F32, name="win%d" % h)
+            nc.vector.memset(wt[:], 0.0)
+            win.append(wt)
+
+        g4 = held.tile([P, 4, SLOTS], F32, name="g4")
+        for j in range(3):
+            nc.vector.tensor_copy(g4[:, j, :], plane[j][:].indirect(offs_t[:]))
+
+        g = [held.tile([P, 4 * C], BF16, name="g%d" % e, align_bytes=64) for e in range(2)]
+        g.append(held.tile([P, 8 * C], BF16, name="g23", align_bytes=64))
+        cod = [held.tile([P, C], U32, name="cod%d" % e, align_bytes=64) for e in range(2)]
+        cod.append(held.tile([P, 2 * C], U32, name="cod23", align_bytes=64))
+        scl = [held.tile([P, C], U8, name="scl%d" % e, align_bytes=64) for e in range(2)]
+        scl.append(held.tile([P, 2 * C], U8, name="scl23", align_bytes=64))
+
+        def gather3(e0, e1):
+            nc.vector.tensor_copy(g4[:, 3, e0 * C : e1 * C], plane[3][:].indirect(offs_t[:, e0 * OC : e1 * OC]))
+
+        def inter(e):
+            dst = g[min(e, 2)][:, max(e - 2, 0) * 4 * C : (max(e - 2, 0) + 1) * 4 * C]
+            nc.scalar.copy(
+                out=dst.rearrange("p (c i j) -> p c j i", i=4, j=4),
+                in_=g4[:, :, e * C : (e + 1) * C].rearrange("p j (c i) -> p c j i", i=4),
+            )
+
+        def quant(i):
+            nc.vector.quantize_mx(out=cod[i][:].bitcast(FP8X4), scales=scl[i][:], in_=g[i][:])
+
+        acc = {}
+
+        def mm(e):
+            i, lo = min(e, 2), max(e - 2, 0) * C
+            for h in range(2):
+                a = psum.tile([P, C], F32, name="acc%d_%d" % (e, h))
+                nc.tensor.matmul_mx(
+                    out=a[:],
+                    lhsT=w_cod[e][:, h * P : (h + 1) * P].bitcast(FP8X4),
+                    lhsT_scale=w_scl[:, e * N + h * P : e * N + (h + 1) * P],
+                    rhs=cod[i][:, lo : lo + C].bitcast(FP8X4),
+                    rhs_scale=scl[i][:, lo : lo + C],
+                    start=True,
+                    stop=True,
+                )
+                acc[(e, h)] = a
+
+        y = {}
+        for h in range(2):
+            for e in range(2):
+                y[(e, h)] = held.tile([P, C], F32, name="y%d_%d" % (e, h))
+            y[(2, h)] = held.tile([P, 2 * C], F32, name="y23_%d" % h)
+
+        def act(e, h):
+            i, lo = min(e, 2), max(e - 2, 0) * C
+            nc.scalar.activation(
+                y[(i, h)][:, lo : lo + C], acc[(e, h)][:], RELU, bias=bias[:, h * E + e : h * E + e + 1], scale=1.0
+            )
+
+        def act_v(e, h):
+            nc.vector.tensor_scalar(
+                y[(e, h)][:], acc[(e, h)][:], bias[:, h * E + e : h * E + e + 1], 0.0,
+                mybir.AluOpType.add, mybir.AluOpType.max,
+            )
+
+        def scat(i, h):
+            lo, hi = (i * OC, (i + 1) * OC) if i < 2 else (2 * OC, 4 * OC)
+            nc.vector.tensor_copy(win[h][:].indirect(offs_t[:, lo:hi]), y[(i, h)][:])
+
+        gather3(0, 1)
+        inter(0)
+        gather3(1, 2)
+        inter(1)
+        gather3(2, 3)
+        quant(0)
+        mm(0)
+        act_v(0, 0)
+        act_v(0, 1)
+        gather3(3, 4)
+        quant(1)
+        mm(1)
+        act(1, 0)
+        act(1, 1)
+        scat(0, 0)
+        inter(2)
+        inter(3)
+        scat(0, 1)
+        quant(2)
+        mm(2)
+        mm(3)
+        act(2, 0)
+        act(3, 0)
+        act(2, 1)
+        act(3, 1)
+        scat(1, 0)
+        scat(1, 1)
+        scat(2, 0)
+        nc.sync.dma_start(out=out[0:P, :], in_=win[0][:])
+        scat(2, 1)
+        nc.sync.dma_start(out=out[P : 2 * P, :], in_=win[1][:])

@@ -17,6 +17,7 @@ RELU = mybir.ActivationFunctionType.Relu
 P = 128
 SLOTS = E * C
 OC = C // 16
+COPY = mybir.ActivationFunctionType.Copy
 
 
 def tile_routed_moe_kernel(tc, xT, w_words, w_scales, b, offs, out):
@@ -31,9 +32,9 @@ def tile_routed_moe_kernel(tc, xT, w_words, w_scales, b, offs, out):
         xv = xT.rearrange("(p j) t -> p j t", j=4)
         plane = []
         for j in range(4):
-            pl = held.tile([P, T], F32, name="plane%d" % j)
-            nc.sync.dma_start(out=pl[:], in_=xv[:, j, :])
-            plane.append(pl)
+            plane.append(held.tile([P, T], F32, name="plane%d" % j))
+        for j in (1, 0, 2, 3):
+            nc.sync.dma_start(out=plane[j][:], in_=xv[:, j, :])
 
         warm = held.tile([P, 2], F32, name="warm")
         nc.vector.memset(warm[:], 0.0)
@@ -67,8 +68,11 @@ def tile_routed_moe_kernel(tc, xT, w_words, w_scales, b, offs, out):
             nc.vector.memset(wt[:], 0.0)
             win.append(wt)
 
+        b0 = held.tile([P, T], BF16, name="b0")
+        nc.vector.tensor_copy(out=b0[:], in_=plane[0][:])
+
         g4 = held.tile([P, 4, SLOTS], F32, name="g4")
-        for j in range(3):
+        for j in range(1, 3):
             nc.vector.tensor_copy(g4[:, j, :], plane[j][:].indirect(offs_t[:]))
 
         g = [held.tile([P, 4 * C], BF16, name="g%d" % e, align_bytes=64) for e in range(2)]
@@ -78,14 +82,23 @@ def tile_routed_moe_kernel(tc, xT, w_words, w_scales, b, offs, out):
         scl = [held.tile([P, C], U8, name="scl%d" % e, align_bytes=64) for e in range(2)]
         scl.append(held.tile([P, 2 * C], U8, name="scl23", align_bytes=64))
 
+        def gather0(i):
+            lo, hi = (i * OC, (i + 1) * OC) if i < 2 else (2 * OC, 4 * OC)
+            nc.scalar.activation(
+                g[i][:].rearrange("p (c j) -> p c j", j=4)[:, :, 0], b0[:].indirect(offs_t[:, lo:hi]), COPY
+            )
+
+        for i in range(3):
+            gather0(i)
+
         def gather3(e0, e1):
             nc.vector.tensor_copy(g4[:, 3, e0 * C : e1 * C], plane[3][:].indirect(offs_t[:, e0 * OC : e1 * OC]))
 
         def inter(e):
             dst = g[min(e, 2)][:, max(e - 2, 0) * 4 * C : (max(e - 2, 0) + 1) * 4 * C]
             nc.scalar.copy(
-                out=dst.rearrange("p (c i j) -> p c j i", i=4, j=4),
-                in_=g4[:, :, e * C : (e + 1) * C].rearrange("p j (c i) -> p c j i", i=4),
+                out=dst.rearrange("p (c i j) -> p c j i", i=4, j=4)[:, :, 1:4, :],
+                in_=g4[:, 1:4, e * C : (e + 1) * C].rearrange("p j (c i) -> p c j i", i=4),
             )
 
         def quant(i):

@@ -69,11 +69,12 @@ def tile_routed_moe_kernel(tc, xT, w_words, w_scales, b, offs, out):
             win.append(wt)
 
         b0 = held.tile([P, T], BF16, name="b0")
-        nc.vector.tensor_copy(out=b0[:], in_=plane[0][:])
+        nc.scalar.copy(out=b0[:], in_=plane[0][:])
 
         g4 = held.tile([P, 4, SLOTS], F32, name="g4")
-        for j in range(1, 3):
-            nc.vector.tensor_copy(g4[:, j, :], plane[j][:].indirect(offs_t[:]))
+        nc.vector.tensor_copy(g4[:, 1, :], plane[1][:].indirect(offs_t[:]))
+        nc.vector.tensor_copy(g4[:, 0, 0 : 3 * C], plane[0][:].indirect(offs_t[:, 0 : 3 * OC]))
+        nc.vector.tensor_copy(g4[:, 2, :], plane[2][:].indirect(offs_t[:]))
 
         g = [held.tile([P, 4 * C], BF16, name="g%d" % e, align_bytes=64) for e in range(2)]
         g.append(held.tile([P, 8 * C], BF16, name="g23", align_bytes=64))
@@ -82,23 +83,21 @@ def tile_routed_moe_kernel(tc, xT, w_words, w_scales, b, offs, out):
         scl = [held.tile([P, C], U8, name="scl%d" % e, align_bytes=64) for e in range(2)]
         scl.append(held.tile([P, 2 * C], U8, name="scl23", align_bytes=64))
 
-        def gather0(i):
-            lo, hi = (i * OC, (i + 1) * OC) if i < 2 else (2 * OC, 4 * OC)
-            nc.scalar.activation(
-                g[i][:].rearrange("p (c j) -> p c j", j=4)[:, :, 0], b0[:].indirect(offs_t[:, lo:hi]), COPY
-            )
-
-        for i in range(3):
-            gather0(i)
+        nc.scalar.activation(
+            g[2][:, 4 * C : 8 * C].rearrange("p (c j) -> p c j", j=4)[:, :, 0],
+            b0[:].indirect(offs_t[:, 3 * OC : 4 * OC]),
+            COPY,
+        )
 
         def gather3(e0, e1):
             nc.vector.tensor_copy(g4[:, 3, e0 * C : e1 * C], plane[3][:].indirect(offs_t[:, e0 * OC : e1 * OC]))
 
         def inter(e):
             dst = g[min(e, 2)][:, max(e - 2, 0) * 4 * C : (max(e - 2, 0) + 1) * 4 * C]
+            j0 = 1 if e == 3 else 0
             nc.scalar.copy(
-                out=dst.rearrange("p (c i j) -> p c j i", i=4, j=4)[:, :, 1:4, :],
-                in_=g4[:, 1:4, e * C : (e + 1) * C].rearrange("p j (c i) -> p c j i", i=4),
+                out=dst.rearrange("p (c i j) -> p c j i", i=4, j=4)[:, :, j0:4, :],
+                in_=g4[:, j0:4, e * C : (e + 1) * C].rearrange("p j (c i) -> p c j i", i=4),
             )
 
         def quant(i):

@@ -79,7 +79,6 @@ def tile_routed_moe_kernel(tc, xT, w_words, w_scales, b, offs, out):
         g = [held.tile([P, 4 * C], BF16, name="g%d" % e, align_bytes=64) for e in range(2)]
         g.append(held.tile([P, 8 * C], BF16, name="g23", align_bytes=64))
         cod = [held.tile([P, C], U32, name="cod%d" % e, align_bytes=64) for e in range(2)]
-        cod.append(held.tile([P, 2 * C], U32, name="cod23", align_bytes=64))
         scl = [held.tile([P, C], U8, name="scl%d" % e, align_bytes=64) for e in range(2)]
         scl.append(held.tile([P, 2 * C], U8, name="scl23", align_bytes=64))
 
@@ -92,12 +91,11 @@ def tile_routed_moe_kernel(tc, xT, w_words, w_scales, b, offs, out):
         def gather3(e0, e1):
             nc.vector.tensor_copy(g4[:, 3, e0 * C : e1 * C], plane[3][:].indirect(offs_t[:, e0 * OC : e1 * OC]))
 
-        def inter(e):
+        def inter(e, j0, j1):
             dst = g[min(e, 2)][:, max(e - 2, 0) * 4 * C : (max(e - 2, 0) + 1) * 4 * C]
-            j0 = 1 if e == 3 else 0
             nc.scalar.copy(
-                out=dst.rearrange("p (c i j) -> p c j i", i=4, j=4)[:, :, j0:4, :],
-                in_=g4[:, j0:4, e * C : (e + 1) * C].rearrange("p j (c i) -> p c j i", i=4),
+                out=dst.rearrange("p (c i j) -> p c j i", i=4, j=4)[:, :, j0:j1, :],
+                in_=g4[:, j0:j1, e * C : (e + 1) * C].rearrange("p j (c i) -> p c j i", i=4),
             )
 
         def quant(i):
@@ -121,9 +119,10 @@ def tile_routed_moe_kernel(tc, xT, w_words, w_scales, b, offs, out):
                 acc[(e, h)] = a
 
         y = {}
+        y[(0, 0)] = held.tile([P, C], F32, name="y0_0", tag="slot_a", align_bytes=64)
+        y[(0, 1)] = held.tile([P, C], F32, name="y0_1")
         for h in range(2):
-            for e in range(2):
-                y[(e, h)] = held.tile([P, C], F32, name="y%d_%d" % (e, h))
+            y[(1, h)] = held.tile([P, C], F32, name="y1_%d" % h)
             y[(2, h)] = held.tile([P, 2 * C], F32, name="y23_%d" % h)
 
         def act(e, h):
@@ -142,10 +141,12 @@ def tile_routed_moe_kernel(tc, xT, w_words, w_scales, b, offs, out):
             lo, hi = (i * OC, (i + 1) * OC) if i < 2 else (2 * OC, 4 * OC)
             nc.vector.tensor_copy(win[h][:].indirect(offs_t[:, lo:hi]), y[(i, h)][:])
 
+        inter(0, 0, 2)
+        inter(1, 0, 2)
         gather3(0, 1)
-        inter(0)
+        inter(0, 2, 4)
         gather3(1, 2)
-        inter(1)
+        inter(1, 2, 4)
         gather3(2, 3)
         quant(0)
         mm(0)
@@ -157,10 +158,11 @@ def tile_routed_moe_kernel(tc, xT, w_words, w_scales, b, offs, out):
         act(1, 0)
         act(1, 1)
         scat(0, 0)
-        inter(2)
-        inter(3)
-        scat(0, 1)
+        inter(2, 0, 4)
+        inter(3, 1, 4)
+        cod.append(held.tile([P, 2 * C], U32, name="cod23", tag="slot_a", align_bytes=64))
         quant(2)
+        scat(0, 1)
         mm(2)
         mm(3)
         act(2, 0)

@@ -62,11 +62,9 @@ def tile_routed_moe_kernel(tc, xT, w_words, w_scales, b, offs, out):
         for e in range(1, E):
             load_w(e)
 
-        win = []
-        for h in range(2):
-            wt = held.tile([P, T], F32, name="win%d" % h)
-            nc.vector.memset(wt[:], 0.0)
-            win.append(wt)
+        win = [held.tile([P, T], F32, name="win%d" % h) for h in range(2)]
+        nc.vector.memset(win[0][:], 0.0)
+        nc.scalar.copy(out=win[1][:], in_=win[0][:])
 
         b0 = held.tile([P, T], BF16, name="b0")
         nc.scalar.copy(out=b0[:], in_=plane[0][:])
@@ -151,7 +149,7 @@ def tile_routed_moe_kernel(tc, xT, w_words, w_scales, b, offs, out):
         quant(0)
         mm(0)
         act_v(0, 0)
-        act_v(0, 1)
+        act(0, 1)
         gather3(3, 4)
         quant(1)
         mm(1)

@@ -67,7 +67,7 @@ def tile_routed_moe_kernel(tc, xT, w_words, w_scales, b, offs, out):
         nc.scalar.copy(out=win[1][:], in_=win[0][:])
 
         b0 = held.tile([P, T], BF16, name="b0")
-        nc.scalar.copy(out=b0[:], in_=plane[0][:])
+        nc.gpsimd.tensor_scalar(b0[:], plane[0][:], 1.0, 0.0, mybir.AluOpType.mult, mybir.AluOpType.add)
 
         g4 = held.tile([P, 4, SLOTS], F32, name="g4")
         nc.vector.tensor_copy(g4[:, 1, :], plane[1][:].indirect(offs_t[:]))

@@ -69,10 +69,8 @@ def tile_routed_moe_kernel(tc, xT, w_words, w_scales, b, offs, out):
         b0 = held.tile([P, T], BF16, name="b0")
         nc.gpsimd.tensor_scalar(b0[:], plane[0][:], 1.0, 0.0, mybir.AluOpType.mult, mybir.AluOpType.add)
 
-        g4 = held.tile([P, 4, SLOTS], F32, name="g4")
-        nc.vector.tensor_copy(g4[:, 1, :], plane[1][:].indirect(offs_t[:]))
-        nc.vector.tensor_copy(g4[:, 0, 0 : 3 * C], plane[0][:].indirect(offs_t[:, 0 : 3 * OC]))
-        nc.vector.tensor_copy(g4[:, 2, :], plane[2][:].indirect(offs_t[:]))
+        b3 = held.tile([P, T], BF16, name="b3")
+        nc.gpsimd.tensor_scalar(b3[:], plane[3][:], 1.0, 0.0, mybir.AluOpType.mult, mybir.AluOpType.add)
 
         g = [held.tile([P, 4 * C], BF16, name="g%d" % e, align_bytes=64) for e in range(2)]
         g.append(held.tile([P, 8 * C], BF16, name="g23", align_bytes=64))
@@ -80,18 +78,20 @@ def tile_routed_moe_kernel(tc, xT, w_words, w_scales, b, offs, out):
         scl = [held.tile([P, C], U8, name="scl%d" % e, align_bytes=64) for e in range(2)]
         scl.append(held.tile([P, 2 * C], U8, name="scl23", align_bytes=64))
 
-        nc.scalar.activation(
-            g[2][:, 4 * C : 8 * C].rearrange("p (c j) -> p c j", j=4)[:, :, 0],
-            b0[:].indirect(offs_t[:, 3 * OC : 4 * OC]),
-            COPY,
-        )
+        def lst(e0, e1):
+            return offs_t[:, e0 * OC : e1 * OC]
 
-        def gather3(e0, e1):
-            nc.vector.tensor_copy(g4[:, 3, e0 * C : e1 * C], plane[3][:].indirect(offs_t[:, e0 * OC : e1 * OC]))
+        def column(t, j):
+            return t.rearrange("p (c j) -> p c j", j=4)[:, :, j]
 
-        def inter(e, j0, j1):
+        g4 = held.tile([P, 4, SLOTS], F32, name="g4")
+        nc.vector.tensor_copy(g4[:, 1, :], plane[1][:].indirect(offs_t[:]))
+        nc.vector.tensor_copy(g4[:, 0, 0 : 3 * C], plane[0][:].indirect(lst(0, 3)))
+        nc.vector.tensor_copy(g4[:, 2, :], plane[2][:].indirect(offs_t[:]))
+
+        def inter(e, j0, j1, eng_copy):
             dst = g[min(e, 2)][:, max(e - 2, 0) * 4 * C : (max(e - 2, 0) + 1) * 4 * C]
-            nc.scalar.copy(
+            eng_copy(
                 out=dst.rearrange("p (c i j) -> p c j i", i=4, j=4)[:, :, j0:j1, :],
                 in_=g4[:, j0:j1, e * C : (e + 1) * C].rearrange("p j (c i) -> p c j i", i=4),
             )
@@ -101,9 +101,9 @@ def tile_routed_moe_kernel(tc, xT, w_words, w_scales, b, offs, out):
 
         acc = {}
 
-        def mm(e):
+        def mm(e, hs):
             i, lo = min(e, 2), max(e - 2, 0) * C
-            for h in range(2):
+            for h in hs:
                 a = psum.tile([P, C], F32, name="acc%d_%d" % (e, h))
                 nc.tensor.matmul_mx(
                     out=a[:],
@@ -129,40 +129,38 @@ def tile_routed_moe_kernel(tc, xT, w_words, w_scales, b, offs, out):
                 y[(i, h)][:, lo : lo + C], acc[(e, h)][:], RELU, bias=bias[:, h * E + e : h * E + e + 1], scale=1.0
             )
 
-        def act_v(e, h):
-            nc.vector.tensor_scalar(
-                y[(e, h)][:], acc[(e, h)][:], bias[:, h * E + e : h * E + e + 1], 0.0,
-                mybir.AluOpType.add, mybir.AluOpType.max,
-            )
-
         def scat(i, h):
-            lo, hi = (i * OC, (i + 1) * OC) if i < 2 else (2 * OC, 4 * OC)
-            nc.vector.tensor_copy(win[h][:].indirect(offs_t[:, lo:hi]), y[(i, h)][:])
+            lo, hi = (i, i + 1) if i < 2 else (2, 4)
+            nc.vector.tensor_copy(win[h][:].indirect(lst(lo, hi)), y[(i, h)][:])
 
-        inter(0, 0, 2)
-        inter(1, 0, 2)
-        gather3(0, 1)
-        inter(0, 2, 4)
-        gather3(1, 2)
-        inter(1, 2, 4)
-        gather3(2, 3)
-        quant(0)
-        mm(0)
-        act_v(0, 0)
+        inter(0, 0, 2, nc.scalar.copy)
+        inter(1, 0, 2, nc.scalar.copy)
+        nc.scalar.activation(column(g[2][:, 4 * C : 8 * C], 0), b0[:].indirect(lst(3, 4)), COPY)
+        for e in range(2):
+            nc.vector.tensor_copy(g4[:, 3, e * C : (e + 1) * C], plane[3][:].indirect(lst(e, e + 1)))
+        for e in range(2):
+            inter(e, 2, 4, nc.vector.tensor_copy)
+        for e in range(2):
+            quant(e)
+        mm(0, (0, 1))
+        nc.vector.tensor_scalar(
+            y[(0, 0)][:], acc[(0, 0)][:], bias[:, 0:1], 0.0, mybir.AluOpType.add, mybir.AluOpType.max
+        )
         act(0, 1)
-        gather3(3, 4)
-        quant(1)
-        mm(1)
+        mm(1, (0, 1))
         act(1, 0)
         act(1, 1)
         scat(0, 0)
-        inter(2, 0, 4)
-        inter(3, 1, 4)
+        nc.scalar.activation(column(g[2][:], 3), b3[:].indirect(lst(2, 4)), COPY)
+        inter(2, 0, 3, nc.scalar.copy)
+        inter(3, 1, 3, nc.scalar.copy)
         cod.append(held.tile([P, 2 * C], U32, name="cod23", tag="slot_a", align_bytes=64))
         quant(2)
         scat(0, 1)
-        mm(2)
-        mm(3)
+        mm(2, (0,))
+        mm(3, (0,))
+        mm(2, (1,))
+        mm(3, (1,))
         act(2, 0)
         act(3, 0)
         act(2, 1)

@@ -146,7 +146,9 @@ def tile_routed_moe_kernel(tc, xT, w_words, w_scales, b, offs, out):
         nc.vector.tensor_scalar(
             y[(0, 0)][:], acc[(0, 0)][:], bias[:, 0:1], 0.0, mybir.AluOpType.add, mybir.AluOpType.max
         )
-        act(0, 1)
+        nc.vector.tensor_scalar(
+            y[(0, 1)][:], acc[(0, 1)][:], bias[:, E : E + 1], 0.0, mybir.AluOpType.add, mybir.AluOpType.max
+        )
         mm(1, (0, 1))
         act(1, 0)
         act(1, 1)

@@ -70,7 +70,8 @@ def tile_routed_moe_kernel(tc, xT, w_words, w_scales, b, offs, out):
         nc.gpsimd.tensor_scalar(b0[:], plane[0][:], 1.0, 0.0, mybir.AluOpType.mult, mybir.AluOpType.add)
 
         b3 = held.tile([P, T], BF16, name="b3")
-        nc.gpsimd.tensor_scalar(b3[:], plane[3][:], 1.0, 0.0, mybir.AluOpType.mult, mybir.AluOpType.add)
+        HT = T // 2
+        nc.gpsimd.tensor_scalar(b3[:, 0:HT], plane[3][:, 0:HT], 1.0, 0.0, mybir.AluOpType.mult, mybir.AluOpType.add)
 
         g = [held.tile([P, 4 * C], BF16, name="g%d" % e, align_bytes=64) for e in range(2)]
         g.append(held.tile([P, 8 * C], BF16, name="g23", align_bytes=64))
@@ -136,6 +137,7 @@ def tile_routed_moe_kernel(tc, xT, w_words, w_scales, b, offs, out):
         inter(0, 0, 2, nc.scalar.copy)
         inter(1, 0, 2, nc.scalar.copy)
         nc.scalar.activation(column(g[2][:, 4 * C : 8 * C], 0), b0[:].indirect(lst(3, 4)), COPY)
+        nc.scalar.copy(out=b3[:, HT:T], in_=plane[3][:, HT:T])
         for e in range(2):
             nc.vector.tensor_copy(g4[:, 3, e * C : (e + 1) * C], plane[3][:].indirect(lst(e, e + 1)))
         for e in range(2):

@@ -27,7 +27,6 @@ def tile_routed_moe_kernel(tc, xT, w_words, w_scales, b, offs, out):
         psum = ctx.enter_context(tc.psum_pool(name="psum", bufs=1))
 
         offs_t = held.tile([P, SLOTS // 16], U16, name="offs_t")
-        nc.sync.dma_start(offs_t[:], offs)
 
         xv = xT.rearrange("(p j) t -> p j t", j=4)
         plane = []
@@ -35,6 +34,8 @@ def tile_routed_moe_kernel(tc, xT, w_words, w_scales, b, offs, out):
             plane.append(held.tile([P, T], F32, name="plane%d" % j))
         for j in (1, 0, 2, 3):
             nc.sync.dma_start(out=plane[j][:], in_=xv[:, j, :])
+            if j == 1:
+                nc.sync.dma_start(offs_t[:], offs)
 
         warm = held.tile([P, 2], F32, name="warm")
         nc.vector.memset(warm[:], 0.0)

@@ -32,10 +32,13 @@ def tile_routed_moe_kernel(tc, xT, w_words, w_scales, b, offs, out):
         plane = []
         for j in range(4):
             plane.append(held.tile([P, T], F32, name="plane%d" % j))
-        for j in (1, 0, 2, 3):
+        for j in (1, 0, 2):
             nc.sync.dma_start(out=plane[j][:], in_=xv[:, j, :])
             if j == 1:
                 nc.sync.dma_start(offs_t[:], offs)
+        HT = T // 2
+        for lo in (0, HT):
+            nc.sync.dma_start(out=plane[3][:, lo : lo + HT], in_=xv[:, 3, lo : lo + HT])
 
         warm = held.tile([P, 2], F32, name="warm")
         nc.vector.memset(warm[:], 0.0)
@@ -43,12 +46,15 @@ def tile_routed_moe_kernel(tc, xT, w_words, w_scales, b, offs, out):
         w_scl = held.tile([P, E * N], U8, name="w_scl", align_bytes=64)
         nc.vector.memset(w_scl[:].bitcast(I32), 0)
 
-        w_cod = [held.tile([P, N], I32, name="w_cod%d" % e, align_bytes=64) for e in range(E)]
+        w_cod = held.tile([P, E * N], I32, name="w_cod", align_bytes=64)
 
-        def load_w(e):
-            nc.sync.dma_start(out=w_cod[e][:], in_=w_words[e, 0].rearrange("p n r -> p (n r)").bitcast(I32))
+        def load_w(e0, e1):
+            nc.sync.dma_start(
+                out=w_cod[:, e0 * N : e1 * N].rearrange("p (e n) -> p e n", n=N),
+                in_=w_words[e0:e1].rearrange("e a p n r -> p e (a n r)").bitcast(I32),
+            )
 
-        load_w(0)
+        load_w(0, 1)
         sv = w_scales.rearrange("e a (q r) n -> r q e (a n)", r=4)
         for r in range(4):
             nc.sync.dma_start(
@@ -60,8 +66,8 @@ def tile_routed_moe_kernel(tc, xT, w_words, w_scales, b, offs, out):
             out=bias[:].rearrange("p (h e) -> p h e", h=2),
             in_=b.rearrange("(h p) e -> p h e", p=P),
         )
-        for e in range(1, E):
-            load_w(e)
+        load_w(1, 2)
+        load_w(2, 4)
 
         win = [held.tile([P, T], F32, name="win%d" % h) for h in range(2)]
         nc.vector.memset(win[0][:], 0.0)
@@ -71,8 +77,9 @@ def tile_routed_moe_kernel(tc, xT, w_words, w_scales, b, offs, out):
         nc.gpsimd.tensor_scalar(b0[:], plane[0][:], 1.0, 0.0, mybir.AluOpType.mult, mybir.AluOpType.add)
 
         b3 = held.tile([P, T], BF16, name="b3")
-        HT = T // 2
-        nc.gpsimd.tensor_scalar(b3[:, 0:HT], plane[3][:, 0:HT], 1.0, 0.0, mybir.AluOpType.mult, mybir.AluOpType.add)
+        QT = 3 * T // 4
+        for lo, hi in ((0, HT), (HT, QT)):
+            nc.gpsimd.tensor_scalar(b3[:, lo:hi], plane[3][:, lo:hi], 1.0, 0.0, mybir.AluOpType.mult, mybir.AluOpType.add)
 
         g = [held.tile([P, 4 * C], BF16, name="g%d" % e, align_bytes=64) for e in range(2)]
         g.append(held.tile([P, 8 * C], BF16, name="g23", align_bytes=64))
@@ -109,7 +116,7 @@ def tile_routed_moe_kernel(tc, xT, w_words, w_scales, b, offs, out):
                 a = psum.tile([P, C], F32, name="acc%d_%d" % (e, h))
                 nc.tensor.matmul_mx(
                     out=a[:],
-                    lhsT=w_cod[e][:, h * P : (h + 1) * P].bitcast(FP8X4),
+                    lhsT=w_cod[:, e * N + h * P : e * N + (h + 1) * P].bitcast(FP8X4),
                     lhsT_scale=w_scl[:, e * N + h * P : e * N + (h + 1) * P],
                     rhs=cod[i][:, lo : lo + C].bitcast(FP8X4),
                     rhs_scale=scl[i][:, lo : lo + C],
@@ -138,7 +145,7 @@ def tile_routed_moe_kernel(tc, xT, w_words, w_scales, b, offs, out):
         inter(0, 0, 2, nc.scalar.copy)
         inter(1, 0, 2, nc.scalar.copy)
         nc.scalar.activation(column(g[2][:, 4 * C : 8 * C], 0), b0[:].indirect(lst(3, 4)), COPY)
-        nc.scalar.copy(out=b3[:, HT:T], in_=plane[3][:, HT:T])
+        nc.scalar.copy(out=b3[:, QT:T], in_=plane[3][:, QT:T])
         for e in range(2):
             nc.vector.tensor_copy(g4[:, 3, e * C : (e + 1) * C], plane[3][:].indirect(lst(e, e + 1)))
         for e in range(2):

@@ -96,7 +96,8 @@ def tile_routed_moe_kernel(tc, xT, w_words, w_scales, b, offs, out):
         g4 = held.tile([P, 4, SLOTS], F32, name="g4")
         nc.vector.tensor_copy(g4[:, 1, :], plane[1][:].indirect(offs_t[:]))
         nc.vector.tensor_copy(g4[:, 0, 0 : 3 * C], plane[0][:].indirect(lst(0, 3)))
-        nc.vector.tensor_copy(g4[:, 2, :], plane[2][:].indirect(offs_t[:]))
+        nc.vector.tensor_copy(column(g[0][:], 2), plane[2][:].indirect(lst(0, 1)))
+        nc.vector.tensor_copy(g4[:, 2, C:SLOTS], plane[2][:].indirect(lst(1, E)))
 
         def inter(e, j0, j1, eng_copy):
             dst = g[min(e, 2)][:, max(e - 2, 0) * 4 * C : (max(e - 2, 0) + 1) * 4 * C]
@@ -146,10 +147,9 @@ def tile_routed_moe_kernel(tc, xT, w_words, w_scales, b, offs, out):
         inter(1, 0, 2, nc.scalar.copy)
         nc.scalar.activation(column(g[2][:, 4 * C : 8 * C], 0), b0[:].indirect(lst(3, 4)), COPY)
         nc.scalar.copy(out=b3[:, QT:T], in_=plane[3][:, QT:T])
-        for e in range(2):
-            nc.vector.tensor_copy(g4[:, 3, e * C : (e + 1) * C], plane[3][:].indirect(lst(e, e + 1)))
-        for e in range(2):
-            inter(e, 2, 4, nc.vector.tensor_copy)
+        nc.vector.tensor_copy(column(g[0][:], 3), plane[3][:].indirect(lst(0, 1)))
+        nc.vector.tensor_copy(g4[:, 3, C : 2 * C], plane[3][:].indirect(lst(1, 2)))
+        inter(1, 2, 4, nc.vector.tensor_copy)
         for e in range(2):
             quant(e)
         mm(0, (0, 1))

@@ -43,7 +43,7 @@ def tile_routed_moe_kernel(tc, xT, w_words, w_scales, b, offs, out):
         warm = held.tile([P, 2], F32, name="warm")
         nc.vector.memset(warm[:], 0.0)
         nc.scalar.activation(warm[:, 1:2], warm[:, 0:1], RELU)
-        w_scl = held.tile([P, E * N], U8, name="w_scl", align_bytes=64)
+        w_scl = held.tile([P, N], U8, name="w_scl", align_bytes=64)
         nc.vector.memset(w_scl[:].bitcast(I32), 0)
 
         w_cod = held.tile([P, E * N], I32, name="w_cod", align_bytes=64)
@@ -54,13 +54,10 @@ def tile_routed_moe_kernel(tc, xT, w_words, w_scales, b, offs, out):
                 in_=w_words[e0:e1].rearrange("e a p n r -> p e (a n r)").bitcast(I32),
             )
 
+        sv = w_scales.rearrange("e a (q r) n -> q e r (a n)", r=4)
+        for q in range(4):
+            nc.sync.dma_start(out=w_scl[32 * q : 32 * q + 16, :].bitcast(I32), in_=sv[q].bitcast(I32))
         load_w(0, 1)
-        sv = w_scales.rearrange("e a (q r) n -> r q e (a n)", r=4)
-        for r in range(4):
-            nc.sync.dma_start(
-                out=w_scl[r:P:32, :].bitcast(I32).rearrange("q (e n) -> q e n", e=E),
-                in_=sv[r].bitcast(I32),
-            )
         bias = held.tile([P, 2 * E], F32, name="bias")
         nc.sync.dma_start(
             out=bias[:].rearrange("p (h e) -> p h e", h=2),
@@ -68,6 +65,8 @@ def tile_routed_moe_kernel(tc, xT, w_words, w_scales, b, offs, out):
         )
         load_w(1, 2)
         load_w(2, 4)
+        bias1 = held.tile([P, 2 * E], F32, name="bias1", tag="slot_b", align_bytes=64)
+        nc.gpsimd.tensor_copy(bias1[:], bias[:])
 
         win = [held.tile([P, T], F32, name="win%d" % h) for h in range(2)]
         nc.vector.memset(win[0][:], 0.0)
@@ -84,8 +83,7 @@ def tile_routed_moe_kernel(tc, xT, w_words, w_scales, b, offs, out):
         g = [held.tile([P, 4 * C], BF16, name="g%d" % e, align_bytes=64) for e in range(2)]
         g.append(held.tile([P, 8 * C], BF16, name="g23", align_bytes=64))
         cod = [held.tile([P, C], U32, name="cod%d" % e, align_bytes=64) for e in range(2)]
-        scl = [held.tile([P, C], U8, name="scl%d" % e, align_bytes=64) for e in range(2)]
-        scl.append(held.tile([P, 2 * C], U8, name="scl23", align_bytes=64))
+        scl = [held.tile([P, C], U8, name="scl%d" % e, align_bytes=64) for e in range(E)]
 
         def lst(e0, e1):
             return offs_t[:, e0 * OC : e1 * OC]
@@ -106,21 +104,21 @@ def tile_routed_moe_kernel(tc, xT, w_words, w_scales, b, offs, out):
                 in_=g4[:, j0:j1, e * C : (e + 1) * C].rearrange("p j (c i) -> p c j i", i=4),
             )
 
-        def quant(i):
-            nc.vector.quantize_mx(out=cod[i][:].bitcast(FP8X4), scales=scl[i][:], in_=g[i][:])
+        def quant(e):
+            gt = g[e][:] if e < 2 else g[2][:, (e - 2) * 4 * C : (e - 1) * 4 * C]
+            nc.vector.quantize_mx(out=cod[e][:].bitcast(FP8X4), scales=scl[e][:], in_=gt)
 
         acc = {}
 
         def mm(e, hs):
-            i, lo = min(e, 2), max(e - 2, 0) * C
             for h in hs:
                 a = psum.tile([P, C], F32, name="acc%d_%d" % (e, h))
                 nc.tensor.matmul_mx(
                     out=a[:],
                     lhsT=w_cod[:, e * N + h * P : e * N + (h + 1) * P].bitcast(FP8X4),
-                    lhsT_scale=w_scl[:, e * N + h * P : e * N + (h + 1) * P],
-                    rhs=cod[i][:, lo : lo + C].bitcast(FP8X4),
-                    rhs_scale=scl[i][:, lo : lo + C],
+                    lhsT_scale=w_scl[4 * e : P, h * P : (h + 1) * P],
+                    rhs=cod[e][:].bitcast(FP8X4),
+                    rhs_scale=scl[e][:],
                     start=True,
                     stop=True,
                 )
@@ -135,8 +133,9 @@ def tile_routed_moe_kernel(tc, xT, w_words, w_scales, b, offs, out):
 
         def act(e, h):
             i, lo = min(e, 2), max(e - 2, 0) * C
+            bt = bias1 if e == 1 else bias
             nc.scalar.activation(
-                y[(i, h)][:, lo : lo + C], acc[(e, h)][:], RELU, bias=bias[:, h * E + e : h * E + e + 1], scale=1.0
+                y[(i, h)][:, lo : lo + C], acc[(e, h)][:], RELU, bias=bt[:, h * E + e : h * E + e + 1], scale=1.0
             )
 
         def scat(i, h):
@@ -163,19 +162,22 @@ def tile_routed_moe_kernel(tc, xT, w_words, w_scales, b, offs, out):
         act(1, 0)
         act(1, 1)
         scat(0, 0)
-        nc.scalar.activation(column(g[2][:], 3), b3[:].indirect(lst(2, 4)), COPY)
         inter(2, 0, 3, nc.scalar.copy)
         inter(3, 1, 3, nc.scalar.copy)
-        cod.append(held.tile([P, 2 * C], U32, name="cod23", tag="slot_a", align_bytes=64))
+        for e in (2, 3):
+            nc.scalar.activation(
+                column(g[2][:, (e - 2) * 4 * C : (e - 1) * 4 * C], 3), b3[:].indirect(lst(e, e + 1)), COPY
+            )
+        cod.append(held.tile([P, C], U32, name="cod2", tag="slot_a", align_bytes=64))
         quant(2)
         scat(0, 1)
-        mm(2, (0,))
-        mm(3, (0,))
-        mm(2, (1,))
-        mm(3, (1,))
+        mm(2, (0, 1))
         act(2, 0)
-        act(3, 0)
         act(2, 1)
+        cod.append(held.tile([P, C], U32, name="cod3", tag="slot_b", align_bytes=64))
+        quant(3)
+        mm(3, (0, 1))
+        act(3, 0)
         act(3, 1)
         scat(1, 0)
         scat(1, 1)

from contextlib import ExitStack

import concourse.mybir as mybir

K, T, E, C, N = 512, 2048, 4, 256, 256
FLOPS = 2 * K * N * E * C

F32 = mybir.dt.float32
BF16 = mybir.dt.bfloat16
U32 = mybir.dt.uint32
I32 = mybir.dt.int32
U16 = mybir.dt.uint16
U8 = mybir.dt.uint8
FP8X4 = mybir.dt.float8_e4m3fn_x4
RELU = mybir.ActivationFunctionType.Relu

P = 128
SLOTS = E * C
OC = C // 16
COPY = mybir.ActivationFunctionType.Copy


def tile_routed_moe_kernel(tc, xT, w_words, w_scales, b, offs, out):
    nc = tc.nc
    with ExitStack() as ctx:
        held = ctx.enter_context(tc.tile_pool(name="held", bufs=1))
        psum = ctx.enter_context(tc.psum_pool(name="psum", bufs=1))

        offs_t = held.tile([P, SLOTS // 16], U16, name="offs_t")

        xv = xT.rearrange("(p j) t -> p j t", j=4)
        plane = []
        for j in range(4):
            plane.append(held.tile([P, T], F32, name="plane%d" % j))
        for j in (1, 0, 2):
            nc.sync.dma_start(out=plane[j][:], in_=xv[:, j, :])
            if j == 1:
                nc.sync.dma_start(offs_t[:], offs)
        HT = T // 2
        for lo in (0, HT):
            nc.sync.dma_start(out=plane[3][:, lo : lo + HT], in_=xv[:, 3, lo : lo + HT])

        warm = held.tile([P, 2], F32, name="warm")
        nc.vector.memset(warm[:], 0.0)
        nc.scalar.activation(warm[:, 1:2], warm[:, 0:1], RELU)
        w_scl = held.tile([P, N], U8, name="w_scl", align_bytes=64)
        nc.vector.memset(w_scl[:].bitcast(I32), 0)

        w_cod = held.tile([P, E * N], I32, name="w_cod", align_bytes=64)

        def load_w(e0, e1):
            nc.sync.dma_start(
                out=w_cod[:, e0 * N : e1 * N].rearrange("p (e n) -> p e n", n=N),
                in_=w_words[e0:e1].rearrange("e a p n r -> p e (a n r)").bitcast(I32),
            )

        sv = w_scales.rearrange("e a (q r) n -> q e r (a n)", r=4)
        for q in range(4):
            nc.sync.dma_start(out=w_scl[32 * q : 32 * q + 16, :].bitcast(I32), in_=sv[q].bitcast(I32))
        load_w(0, 1)
        bias = held.tile([P, 2 * E], F32, name="bias")
        nc.sync.dma_start(
            out=bias[:].rearrange("p (h e) -> p h e", h=2),
            in_=b.rearrange("(h p) e -> p h e", p=P),
        )
        load_w(1, 2)
        load_w(2, 4)
        bias1 = held.tile([P, 2 * E], F32, name="bias1", tag="slot_b", align_bytes=64)
        nc.gpsimd.tensor_copy(bias1[:], bias[:])

        win = [held.tile([P, T], F32, name="win%d" % h) for h in range(2)]
        nc.vector.memset(win[0][:], 0.0)
        nc.scalar.copy(out=win[1][:], in_=win[0][:])

        b0 = held.tile([P, T], BF16, name="b0")
        nc.gpsimd.tensor_scalar(b0[:], plane[0][:], 1.0, 0.0, mybir.AluOpType.mult, mybir.AluOpType.add)

        b3 = held.tile([P, T], BF16, name="b3")
        QT = 3 * T // 4
        for lo, hi in ((0, HT), (HT, QT)):
            nc.gpsimd.tensor_scalar(b3[:, lo:hi], plane[3][:, lo:hi], 1.0, 0.0, mybir.AluOpType.mult, mybir.AluOpType.add)

        g = [held.tile([P, 4 * C], BF16, name="g%d" % e, align_bytes=64) for e in range(2)]
        g.append(held.tile([P, 8 * C], BF16, name="g23", align_bytes=64))
        cod = [held.tile([P, C], U32, name="cod%d" % e, align_bytes=64) for e in range(2)]
        scl = [held.tile([P, C], U8, name="scl%d" % e, align_bytes=64) for e in range(E)]

        def lst(e0, e1):
            return offs_t[:, e0 * OC : e1 * OC]

        def column(t, j):
            return t.rearrange("p (c j) -> p c j", j=4)[:, :, j]

        g4 = held.tile([P, 4, SLOTS], F32, name="g4")
        nc.vector.tensor_copy(g4[:, 1, :], plane[1][:].indirect(offs_t[:]))
        nc.vector.tensor_copy(g4[:, 0, 0 : 3 * C], plane[0][:].indirect(lst(0, 3)))
        nc.vector.tensor_copy(column(g[0][:], 2), plane[2][:].indirect(lst(0, 1)))
        nc.vector.tensor_copy(g4[:, 2, C:SLOTS], plane[2][:].indirect(lst(1, E)))

        def inter(e, j0, j1, eng_copy):
            dst = g[min(e, 2)][:, max(e - 2, 0) * 4 * C : (max(e - 2, 0) + 1) * 4 * C]
            eng_copy(
                out=dst.rearrange("p (c i j) -> p c j i", i=4, j=4)[:, :, j0:j1, :],
                in_=g4[:, j0:j1, e * C : (e + 1) * C].rearrange("p j (c i) -> p c j i", i=4),
            )

        def quant(e):
            gt = g[e][:] if e < 2 else g[2][:, (e - 2) * 4 * C : (e - 1) * 4 * C]
            nc.vector.quantize_mx(out=cod[e][:].bitcast(FP8X4), scales=scl[e][:], in_=gt)

        acc = {}

        def mm(e, hs):
            for h in hs:
                a = psum.tile([P, C], F32, name="acc%d_%d" % (e, h))
                nc.tensor.matmul_mx(
                    out=a[:],
                    lhsT=w_cod[:, e * N + h * P : e * N + (h + 1) * P].bitcast(FP8X4),
                    lhsT_scale=w_scl[4 * e : P, h * P : (h + 1) * P],
                    rhs=cod[e][:].bitcast(FP8X4),
                    rhs_scale=scl[e][:],
                    start=True,
                    stop=True,
                )
                acc[(e, h)] = a

        y = {}
        y[(0, 0)] = held.tile([P, C], F32, name="y0_0", tag="slot_a", align_bytes=64)
        y[(0, 1)] = held.tile([P, C], F32, name="y0_1")
        for h in range(2):
            y[(1, h)] = held.tile([P, C], F32, name="y1_%d" % h)
            y[(2, h)] = held.tile([P, 2 * C], F32, name="y23_%d" % h)

        def act(e, h):
            i, lo = min(e, 2), max(e - 2, 0) * C
            bt = bias1 if e == 1 else bias
            nc.scalar.activation(
                y[(i, h)][:, lo : lo + C], acc[(e, h)][:], RELU, bias=bt[:, h * E + e : h * E + e + 1], scale=1.0
            )

        def scat(i, h):
            lo, hi = (i, i + 1) if i < 2 else (2, 4)
            nc.vector.tensor_copy(win[h][:].indirect(lst(lo, hi)), y[(i, h)][:])

        inter(0, 0, 2, nc.scalar.copy)
        inter(1, 0, 2, nc.scalar.copy)
        nc.scalar.activation(column(g[2][:, 4 * C : 8 * C], 0), b0[:].indirect(lst(3, 4)), COPY)
        nc.scalar.copy(out=b3[:, QT:T], in_=plane[3][:, QT:T])
        nc.vector.tensor_copy(column(g[0][:], 3), plane[3][:].indirect(lst(0, 1)))
        nc.vector.tensor_copy(g4[:, 3, C : 2 * C], plane[3][:].indirect(lst(1, 2)))
        inter(1, 2, 4, nc.vector.tensor_copy)
        for e in range(2):
            quant(e)
        mm(0, (0, 1))
        nc.vector.tensor_scalar(
            y[(0, 0)][:], acc[(0, 0)][:], bias[:, 0:1], 0.0, mybir.AluOpType.add, mybir.AluOpType.max
        )
        nc.vector.tensor_scalar(
            y[(0, 1)][:], acc[(0, 1)][:], bias[:, E : E + 1], 0.0, mybir.AluOpType.add, mybir.AluOpType.max
        )
        mm(1, (0, 1))
        act(1, 0)
        act(1, 1)
        scat(0, 0)
        inter(2, 0, 3, nc.scalar.copy)
        inter(3, 1, 3, nc.scalar.copy)
        for e in (2, 3):
            nc.scalar.activation(
                column(g[2][:, (e - 2) * 4 * C : (e - 1) * 4 * C], 3), b3[:].indirect(lst(e, e + 1)), COPY
            )
        cod.append(held.tile([P, C], U32, name="cod2", tag="slot_a", align_bytes=64))
        quant(2)
        scat(0, 1)
        mm(2, (0, 1))
        act(2, 0)
        act(2, 1)
        cod.append(held.tile([P, C], U32, name="cod3", tag="slot_b", align_bytes=64))
        quant(3)
        mm(3, (0, 1))
        act(3, 0)
        act(3, 1)
        scat(1, 0)
        scat(1, 1)
        scat(2, 0)
        nc.sync.dma_start(out=out[0:P, :], in_=win[0][:])
        scat(2, 1)
        nc.sync.dma_start(out=out[P : 2 * P, :], in_=win[1][:])
